import numpy as np
import ml_dtypes


def mxq(x, axis, fmt="e4m3"):
    dtype, down = {"e4m3": (ml_dtypes.float8_e4m3fn, 7), "e5m2": (ml_dtypes.float8_e5m2, 14)}[fmt]
    v = np.moveaxis(np.asarray(x, np.float32).astype(ml_dtypes.bfloat16).astype(np.float64), axis, -1)
    blocks = v.reshape(v.shape[:-1] + (-1, 32))
    amax = np.abs(blocks).max(-1, keepdims=True)
    byte = np.maximum(np.where(amax > 0, np.frexp(amax)[1] - 1 + 127, 0) - down, 1)
    scale = np.exp2(byte - 127.0)
    codes = (blocks / scale).astype(np.float32).astype(dtype).astype(np.float64)
    return np.moveaxis((codes * scale).reshape(v.shape), -1, axis)


WIDE = False


def mx_kscale(k):
    if not WIDE:
        return np.ones(k)
    levels = np.array([30, -30])
    if k % 512:
        return np.exp2(np.random.permutation(np.resize(levels, k // 32))).repeat(32)
    a = np.empty((k // 512, 16))
    for p in range(k // 512):
        a[p, :8] = np.random.permutation(np.resize(levels, 8))
        for g in range(8):
            far = levels[np.abs(levels - a[p, g]) >= 10]
            a[p, g + 8] = far[np.random.randint(len(far))]
    return np.exp2(a.ravel()).repeat(32)


def f64(x):
    return np.asarray(x).astype(np.float64)


E2M1 = np.array([0.0, 0.5, 1.0, 1.5, 2.0, 3.0, 4.0, 6.0, -0.0, -0.5, -1.0, -1.5, -2.0, -3.0, -4.0, -6.0])


def pack_weight(w, fmt):
    k, n = w.shape
    w = f64(np.asarray(w, np.float32).astype(ml_dtypes.bfloat16)).reshape(k // 32, 32, n)
    amax = np.abs(w).max(1)
    if fmt == "e4m3":
        byte = np.frexp(amax)[1] - 1 + 127 - 7
    else:
        mant, ex = np.frexp(amax / 6.0)
        byte = np.where(mant > 0.5, ex, ex - 1) + 127
    byte = np.clip(np.where(amax > 0, byte, 1), 1, 254)
    scaled = (w * np.exp2(127.0 - byte)[:, None, :]).reshape(k, n).astype(np.float32)
    by_word = np.ascontiguousarray(scaled.reshape(k // 512, 128, 4, n).transpose(0, 1, 3, 2))
    if fmt == "e4m3":
        words = by_word.astype(ml_dtypes.float8_e4m3fn).view(np.uint8)
    else:
        c = by_word.astype(ml_dtypes.float4_e2m1fn).view(np.uint8) & 0xF
        words = (c[..., 0::2] | (c[..., 1::2] << 4)).reshape(k // 512, 128, 2 * n)
    return np.ascontiguousarray(words), np.ascontiguousarray(byte.astype(np.uint8).reshape(k // 512, 16, n))


def unpack_weight(words, scales, fmt):
    g, _, n = scales.shape
    words = np.ascontiguousarray(words).reshape(g, 128, n, -1)
    if fmt == "e4m3":
        vals = words.view(ml_dtypes.float8_e4m3fn).astype(np.float64)
    else:
        nib = np.empty((g, 128, n, 4), np.uint8)
        nib[..., 0::2] = words & 0xF
        nib[..., 1::2] = words >> 4
        vals = E2M1[nib]
    vals = vals * np.repeat(np.exp2(scales.astype(np.float64) - 127.0), 8, axis=1)[..., None]
    return vals.transpose(0, 1, 3, 2).reshape(g * 512, n)


K, R, T, S, N = 1024, 512, 512, 512, 512


def setup_inputs():
    n = np.random.standard_normal
    fk = mx_kscale(K)
    ft = mx_kscale(T)
    fs = mx_kscale(S)
    xtp = pack_weight(n((K, T)) / fk[:, None], "e4m3")
    wap = pack_weight(n((K, R)) * 1 / np.sqrt(K) * fk[:, None], "e2m1")
    hsp = pack_weight(n((S, R)) * fs[:, None], "e4m3")
    gsp = pack_weight(n((S, N)) / fs[:, None], "e2m1")
    return {
        "xt_words": xtp[0],
        "xt_scales": xtp[1],
        "wa_words": wap[0],
        "wa_scales": wap[1],
        "rw": (np.random.uniform(0.5, 1.5, (1, T)) * ft).astype(np.float32),
        "g": (n((T, N)) * np.exp(0.5 * n((T, 1))) / ft[:, None]).astype(np.float32),
        "hs_words": hsp[0],
        "hs_scales": hsp[1],
        "gs_words": gsp[0],
        "gs_scales": gsp[1],
    }


def reference(xt_words, xt_scales, wa_words, wa_scales, rw, g, hs_words, hs_scales, gs_words, gs_scales):
    xtu = unpack_weight(xt_words, xt_scales, "e4m3")
    wau = unpack_weight(wa_words, wa_scales, "e2m1")
    hsu = unpack_weight(hs_words, hs_scales, "e4m3")
    gsu = unpack_weight(gs_words, gs_scales, "e2m1")
    a = wau.T @ xtu
    h1 = np.maximum(a, 0.0) * f64(rw)
    ht = h1.T
    htq = mxq(ht, 0, "e4m3")
    gq = mxq(f64(g), 0, "e5m2")
    w = htq.T @ gq + hsu.T @ gsu
    y = 0.04 * w
    return y

@@ -1,0 +1,180 @@
+from contextlib import ExitStack
+
+import concourse.mybir as mybir
+
+K, R, T, S, N = 1024, 512, 512, 512, 512
+FLOPS = 2 * (K * R * T + T * R * N + S * R * N)
+
+F32 = mybir.dt.float32
+BF16 = mybir.dt.bfloat16
+I32 = mybir.dt.int32
+U8 = mybir.dt.uint8
+E4M3 = mybir.dt.float8_e4m3fn_x4
+E5M2 = mybir.dt.float8_e5m2_x4
+E2M1 = mybir.dt.float4_e2m1fn_x4
+ALU = mybir.AluOpType
+ACT = mybir.ActivationFunctionType
+
+P = 128
+PACK = 4
+KP = K // (P * PACK)
+RT = R // P
+HALF = N // 2
+OUT_SCALE = 0.04
+
+
+def load_scales(queue, plane, scales, rows):
+    for row in rows:
+        queue.dma_start(
+            out=plane[row:P:32, :, :].bitcast(I32),
+            in_=scales[:, row:16:4, :].rearrange("z q c -> q z c").bitcast(I32),
+        )
+
+
+def tile_mix_wgrad_of_hidden_and_store_kernel(
+    tc, xt_words, xt_scales, wa_words, wa_scales, rw, g, hs_words, hs_scales, gs_words, gs_scales, out
+):
+    nc = tc.nc
+    with ExitStack() as ctx:
+        sb = ctx.enter_context(tc.tile_pool(name="sb", bufs=1))
+        ps = ctx.enter_context(tc.psum_pool(name="ps", bufs=1))
+        ctx.enter_context(tc.manual_schedule())
+
+        xs_raw = sb.tile([P, KP, T], U8, align_bytes=64)
+        ws = sb.tile([P, KP, R], U8, align_bytes=64)
+        hss = sb.tile([P, 1, R], U8, align_bytes=64)
+        gss = sb.tile([P, 1, N], U8, align_bytes=64)
+        for plane in (xs_raw, ws, gss, hss):
+            nc.vector.memset(plane[:].bitcast(I32), 0)
+
+        xt_raw = sb.tile([P, KP, T], I32, align_bytes=64)
+        wa = sb.tile([P, KP, 2 * R], U8, align_bytes=64)
+        rw_sb = sb.tile([P, 1, PACK], F32, align_bytes=64)
+        hs = sb.tile([P, R], I32, align_bytes=64)
+        gs = sb.tile([P, 2 * N], U8, align_bytes=64)
+        g_raw = [sb.tile([P, PACK, HALF], F32, align_bytes=64, name="g_raw%d" % h) for h in range(2)]
+        g_rows = g.rearrange("(p j) n -> p j n", j=PACK)
+
+        load_scales(nc.sync, xs_raw, xt_scales, range(4))
+        nc.sync.dma_start(out=xt_raw[:], in_=xt_words.rearrange("z p c b -> p z (c b)").bitcast(I32))
+        nc.sync.dma_start(out=wa[:].bitcast(I32), in_=wa_words.rearrange("z p c -> p z c").bitcast(I32))
+        load_scales(nc.sync, ws, wa_scales, range(4))
+        nc.sync.dma_start(out=rw_sb[:], in_=rw.rearrange("o (p j) -> p o j", j=PACK))
+        for h in range(2):
+            nc.sync.dma_start(out=g_raw[h][:], in_=g_rows[:, :, h * HALF : (h + 1) * HALF])
+        nc.sync.dma_start(out=hs[:], in_=hs_words[0].rearrange("p c b -> p (c b)").bitcast(I32))
+        nc.sync.dma_start(out=gs[:].bitcast(I32), in_=gs_words[0].bitcast(I32))
+        load_scales(nc.sync, hss, hs_scales, range(4))
+        load_scales(nc.gpsimd, gss, gs_scales, range(4))
+
+        xs = sb.tile([P, KP, PACK, P], U8, align_bytes=64)
+        nc.vector.tensor_copy(
+            out=xs[:].rearrange("p z j m -> p z m j"),
+            in_=xs_raw[:].rearrange("p z (m j) -> p z m j", j=PACK),
+        )
+        xt = sb.tile([P, KP, PACK, P], I32, align_bytes=64)
+        for z in range(KP):
+            nc.vector.tensor_copy(
+                out=xt[:, z, :, :].rearrange("p j (c i) -> p c j i", i=4),
+                in_=xt_raw[:, z, :].rearrange("p (c i j) -> p c j i", i=4, j=PACK),
+            )
+
+        g_bf = [sb.tile([P, HALF, PACK], BF16, align_bytes=64, name="g_bf%d" % h) for h in range(2)]
+        gq = sb.tile([P, N], I32, align_bytes=64)
+        gq_s = sb.tile([P, N], U8, align_bytes=64)
+
+        def g_views(h):
+            return (
+                g_bf[h][:].rearrange("p (c i) j -> p c j i", i=4),
+                g_raw[h][:].rearrange("p j (c i) -> p c j i", i=4),
+            )
+
+        def quantize_g(h):
+            cols = slice(h * HALF, (h + 1) * HALF)
+            nc.vector.quantize_mx(
+                out=gq[:, cols].bitcast(E5M2), scales=gq_s[:, cols], in_=g_bf[h][:].rearrange("p n j -> p (n j)")
+            )
+
+        dst, src = g_views(0)
+        nc.vector.tensor_copy(out=dst, in_=src)
+        dst, src = g_views(1)
+        nc.scalar.activation(out=dst, in_=src, func=ACT.Copy)
+
+        pre = [ps.tile([P, PACK, P], F32, name="pre%d" % b) for b in range(RT)]
+        acc = [ps.tile([P, N], F32, name="acc%d" % b) for b in range(RT)]
+        ht = [sb.tile([P, P, PACK], BF16, align_bytes=64, name="ht%d" % b) for b in range(RT)]
+        hq = [sb.tile([P, P], I32, align_bytes=64, name="hq%d" % b) for b in range(RT)]
+        hq_s = [sb.tile([P, P], U8, align_bytes=64, name="hq_s%d" % b) for b in range(RT)]
+        res = [sb.tile([P, N], F32, align_bytes=64, name="res%d" % b) for b in range(RT)]
+
+        def hidden(b):
+            for j in range(PACK):
+                for z in range(KP):
+                    nc.tensor.matmul_mx(
+                        out=pre[b][:, j, :],
+                        lhsT=xt[:, z, j, :].bitcast(E4M3),
+                        lhsT_scale=xs[:, z, j, :],
+                        rhs=wa[:, z, 2 * b * P : 2 * (b + 1) * P].bitcast(E2M1),
+                        rhs_scale=ws[:, z, b * P : (b + 1) * P],
+                        start=(z == 0),
+                        stop=(z == KP - 1),
+                    )
+
+        def weigh(b):
+            nc.vector.scalar_tensor_tensor(
+                out=ht[b][:],
+                in0=pre[b][:].rearrange("p j r -> p r j"),
+                scalar=0.0,
+                in1=rw_sb[:].to_broadcast([P, P, PACK]),
+                op0=ALU.max,
+                op1=ALU.mult,
+            )
+
+        def quantize_h(b):
+            nc.vector.quantize_mx(
+                out=hq[b][:].bitcast(E4M3), scales=hq_s[b][:], in_=ht[b][:].rearrange("p r j -> p (r j)")
+            )
+
+        def gradient(b):
+            cols = slice(b * P, (b + 1) * P)
+            nc.tensor.matmul_mx(
+                out=acc[b][:],
+                lhsT=hs[:, cols].bitcast(E4M3),
+                lhsT_scale=hss[:, 0, cols],
+                rhs=gs[:].bitcast(E2M1),
+                rhs_scale=gss[:, 0, :],
+                start=True,
+                stop=False,
+            )
+            nc.tensor.matmul_mx(
+                out=acc[b][:],
+                lhsT=hq[b][:].bitcast(E4M3),
+                lhsT_scale=hq_s[b][:],
+                rhs=gq[:].bitcast(E5M2),
+                rhs_scale=gq_s[:],
+                start=False,
+                stop=True,
+            )
+
+        def store(b):
+            if b == RT - 1:
+                nc.vector.tensor_scalar(out=res[b][:], in0=acc[b][:], scalar1=OUT_SCALE, scalar2=None, op0=ALU.mult)
+            else:
+                nc.scalar.activation(out=res[b][:], in_=acc[b][:], func=ACT.Copy, scale=OUT_SCALE)
+            nc.sync.dma_start(out=out[b * P : (b + 1) * P, :], in_=res[b][:])
+
+        for b in range(RT):
+            hidden(b)
+        weigh(0)
+        quantize_g(0)
+        weigh(1)
+        quantize_h(0)
+        quantize_g(1)
+        weigh(2)
+        quantize_h(1)
+        weigh(3)
+        quantize_h(2)
+        quantize_h(3)
+        for b in range(RT):
+            gradient(b)
+            store(b)

@@ -20,6 +20,7 @@ PACK = 4
 KP = K // (P * PACK)
 RT = R // P
 HALF = N // 2
+QUARTER = N // 4
 OUT_SCALE = 0.04
 
 
@@ -42,9 +43,11 @@ def tile_mix_wgrad_of_hidden_and_store_kernel(
 
         xs_raw = sb.tile([P, KP, T], U8, align_bytes=64)
         ws = sb.tile([P, KP, R], U8, align_bytes=64)
-        hss = sb.tile([P, 1, R], U8, align_bytes=64)
-        gss = sb.tile([P, 1, N], U8, align_bytes=64)
-        for plane in (xs_raw, ws, gss, hss):
+        stored_s = sb.tile([P, 2, N], U8, align_bytes=64)
+        staged = sb.tile([16, 2, N], U8, align_bytes=64)
+        nc.gpsimd.dma_start(out=staged[:, 0, :].bitcast(I32), in_=hs_scales[0].bitcast(I32))
+        nc.gpsimd.dma_start(out=staged[:, 1, :].bitcast(I32), in_=gs_scales[0].bitcast(I32))
+        for plane in (xs_raw, ws, stored_s):
             nc.vector.memset(plane[:].bitcast(I32), 0)
 
         xt_raw = sb.tile([P, KP, T], I32, align_bytes=64)
@@ -55,22 +58,23 @@ def tile_mix_wgrad_of_hidden_and_store_kernel(
         g_raw = [sb.tile([P, PACK, HALF], F32, align_bytes=64, name="g_raw%d" % h) for h in range(2)]
         g_rows = g.rearrange("(p j) n -> p j n", j=PACK)
 
-        load_scales(nc.sync, xs_raw, xt_scales, range(4))
+        load_scales(nc.sync, xs_raw, xt_scales, range(2))
+        load_scales(nc.scalar, xs_raw, xt_scales, range(2, 4))
         nc.sync.dma_start(out=xt_raw[:], in_=xt_words.rearrange("z p c b -> p z (c b)").bitcast(I32))
         nc.sync.dma_start(out=wa[:].bitcast(I32), in_=wa_words.rearrange("z p c -> p z c").bitcast(I32))
         load_scales(nc.sync, ws, wa_scales, range(4))
         nc.sync.dma_start(out=rw_sb[:], in_=rw.rearrange("o (p j) -> p o j", j=PACK))
         for h in range(2):
             nc.sync.dma_start(out=g_raw[h][:], in_=g_rows[:, :, h * HALF : (h + 1) * HALF])
-        nc.sync.dma_start(out=hs[:], in_=hs_words[0].rearrange("p c b -> p (c b)").bitcast(I32))
         nc.sync.dma_start(out=gs[:].bitcast(I32), in_=gs_words[0].bitcast(I32))
-        load_scales(nc.sync, hss, hs_scales, range(4))
-        load_scales(nc.gpsimd, gss, gs_scales, range(4))
+        nc.sync.dma_start(out=hs[:], in_=hs_words[0].rearrange("p c b -> p (c b)").bitcast(I32))
+        for row in range(4):
+            nc.sync.dma_start(out=stored_s[row:P:32, :, :].bitcast(I32), in_=staged[row:16:4, :, :].bitcast(I32))
 
         xs = sb.tile([P, KP, PACK, P], U8, align_bytes=64)
         nc.vector.tensor_copy(
-            out=xs[:].rearrange("p z j m -> p z m j"),
-            in_=xs_raw[:].rearrange("p z (m j) -> p z m j", j=PACK),
+            out=xs[:].rearrange("p z j (c i) -> p z c j i", i=16),
+            in_=xs_raw[:].rearrange("p z (c i j) -> p z c j i", i=16, j=PACK),
         )
         xt = sb.tile([P, KP, PACK, P], I32, align_bytes=64)
         for z in range(KP):
@@ -79,25 +83,28 @@ def tile_mix_wgrad_of_hidden_and_store_kernel(
                 in_=xt_raw[:, z, :].rearrange("p (c i j) -> p c j i", i=4, j=PACK),
             )
 
-        g_bf = [sb.tile([P, HALF, PACK], BF16, align_bytes=64, name="g_bf%d" % h) for h in range(2)]
+        g_bf = sb.tile([P, N * PACK], BF16, align_bytes=64)
         gq = sb.tile([P, N], I32, align_bytes=64)
         gq_s = sb.tile([P, N], U8, align_bytes=64)
 
-        def g_views(h):
+        def g_views(h, lo, hi):
+            first = h * HALF
             return (
-                g_bf[h][:].rearrange("p (c i) j -> p c j i", i=4),
-                g_raw[h][:].rearrange("p j (c i) -> p c j i", i=4),
+                g_bf[:, (first + lo) * PACK : (first + hi) * PACK].rearrange("p (c i j) -> p c j i", i=4, j=PACK),
+                g_raw[h][:, :, lo:hi].rearrange("p j (c i) -> p c j i", i=4),
             )
 
         def quantize_g(h):
             cols = slice(h * HALF, (h + 1) * HALF)
             nc.vector.quantize_mx(
-                out=gq[:, cols].bitcast(E5M2), scales=gq_s[:, cols], in_=g_bf[h][:].rearrange("p n j -> p (n j)")
+                out=gq[:, cols].bitcast(E5M2),
+                scales=gq_s[:, cols],
+                in_=g_bf[:, h * HALF * PACK : (h + 1) * HALF * PACK],
             )
 
-        dst, src = g_views(0)
-        nc.vector.tensor_copy(out=dst, in_=src)
-        dst, src = g_views(1)
+        dst, src = g_views(0, 0, HALF)
+        nc.scalar.activation(out=dst, in_=src, func=ACT.Copy)
+        dst, src = g_views(1, 0, QUARTER)
         nc.scalar.activation(out=dst, in_=src, func=ACT.Copy)
 
         pre = [ps.tile([P, PACK, P], F32, name="pre%d" % b) for b in range(RT)]
@@ -135,17 +142,19 @@ def tile_mix_wgrad_of_hidden_and_store_kernel(
                 out=hq[b][:].bitcast(E4M3), scales=hq_s[b][:], in_=ht[b][:].rearrange("p r j -> p (r j)")
             )
 
-        def gradient(b):
+        def stored(b):
             cols = slice(b * P, (b + 1) * P)
             nc.tensor.matmul_mx(
                 out=acc[b][:],
                 lhsT=hs[:, cols].bitcast(E4M3),
-                lhsT_scale=hss[:, 0, cols],
+                lhsT_scale=stored_s[:, 0, cols],
                 rhs=gs[:].bitcast(E2M1),
-                rhs_scale=gss[:, 0, :],
+                rhs_scale=stored_s[:, 1, :],
                 start=True,
                 stop=False,
             )
+
+        def fresh(b):
             nc.tensor.matmul_mx(
                 out=acc[b][:],
                 lhsT=hq[b][:].bitcast(E4M3),
@@ -166,15 +175,18 @@ def tile_mix_wgrad_of_hidden_and_store_kernel(
         for b in range(RT):
             hidden(b)
         weigh(0)
-        quantize_g(0)
         weigh(1)
         quantize_h(0)
+        dst, src = g_views(1, QUARTER, HALF)
+        nc.vector.tensor_copy(out=dst, in_=src)
+        quantize_g(0)
         quantize_g(1)
         weigh(2)
         quantize_h(1)
-        weigh(3)
         quantize_h(2)
+        weigh(3)
         quantize_h(3)
         for b in range(RT):
-            gradient(b)
+            stored(b)
+            fresh(b)
             store(b)

@@ -20,7 +20,7 @@ PACK = 4
 KP = K // (P * PACK)
 RT = R // P
 HALF = N // 2
-QUARTER = N // 4
+SCALAR_COLS = (192, 128)
 OUT_SCALE = 0.04
 
 
@@ -47,8 +47,18 @@ def tile_mix_wgrad_of_hidden_and_store_kernel(
         staged = sb.tile([16, 2, N], U8, align_bytes=64)
         nc.gpsimd.dma_start(out=staged[:, 0, :].bitcast(I32), in_=hs_scales[0].bitcast(I32))
         nc.gpsimd.dma_start(out=staged[:, 1, :].bitcast(I32), in_=gs_scales[0].bitcast(I32))
-        for plane in (xs_raw, ws, stored_s):
-            nc.vector.memset(plane[:].bitcast(I32), 0)
+        nc.vector.memset(xs_raw[:].bitcast(I32), 0)
+        ones = sb.tile([P, P * PACK], BF16, align_bytes=64)
+        warm_a = sb.tile([P, P], I32, align_bytes=64)
+        warm_a_s = sb.tile([P, P], U8, align_bytes=64)
+        warm_b = sb.tile([P, N], I32, align_bytes=64)
+        warm_b_s = sb.tile([P, N], U8, align_bytes=64)
+        nc.vector.memset(ones[:], 1.0)
+        nc.vector.memset(ws[:].bitcast(I32), 0)
+        nc.vector.quantize_mx(out=warm_a[:].bitcast(E4M3), scales=warm_a_s[:], in_=ones[:])
+        for c in range(0, N, P):
+            nc.vector.quantize_mx(out=warm_b[:, c : c + P].bitcast(E5M2), scales=warm_b_s[:, c : c + P], in_=ones[:])
+        nc.vector.memset(stored_s[:].bitcast(I32), 0)
 
         xt_raw = sb.tile([P, KP, T], I32, align_bytes=64)
         wa = sb.tile([P, KP, 2 * R], U8, align_bytes=64)
@@ -67,9 +77,11 @@ def tile_mix_wgrad_of_hidden_and_store_kernel(
         for h in range(2):
             nc.sync.dma_start(out=g_raw[h][:], in_=g_rows[:, :, h * HALF : (h + 1) * HALF])
         nc.sync.dma_start(out=gs[:].bitcast(I32), in_=gs_words[0].bitcast(I32))
-        nc.sync.dma_start(out=hs[:], in_=hs_words[0].rearrange("p c b -> p (c b)").bitcast(I32))
+        hs_cols = hs_words[0].rearrange("p c b -> p (c b)").bitcast(I32)
+        nc.sync.dma_start(out=hs[:, :P], in_=hs_cols[:, :P])
         for row in range(4):
             nc.sync.dma_start(out=stored_s[row:P:32, :, :].bitcast(I32), in_=staged[row:16:4, :, :].bitcast(I32))
+        nc.sync.dma_start(out=hs[:, P:], in_=hs_cols[:, P:])
 
         xs = sb.tile([P, KP, PACK, P], U8, align_bytes=64)
         nc.vector.tensor_copy(
@@ -102,10 +114,13 @@ def tile_mix_wgrad_of_hidden_and_store_kernel(
                 in_=g_bf[:, h * HALF * PACK : (h + 1) * HALF * PACK],
             )
 
-        dst, src = g_views(0, 0, HALF)
-        nc.scalar.activation(out=dst, in_=src, func=ACT.Copy)
-        dst, src = g_views(1, 0, QUARTER)
-        nc.scalar.activation(out=dst, in_=src, func=ACT.Copy)
+        for h in range(2):
+            dst, src = g_views(h, 0, SCALAR_COLS[h])
+            nc.scalar.activation(out=dst, in_=src, func=ACT.Copy)
+
+        def cast_rest(h):
+            dst, src = g_views(h, SCALAR_COLS[h], HALF)
+            nc.vector.tensor_copy(out=dst, in_=src)
 
         pre = [ps.tile([P, PACK, P], F32, name="pre%d" % b) for b in range(RT)]
         acc = [ps.tile([P, N], F32, name="acc%d" % b) for b in range(RT)]
@@ -166,27 +181,42 @@ def tile_mix_wgrad_of_hidden_and_store_kernel(
             )
 
         def store(b):
-            if b == RT - 1:
+            if b == RT - 2:
                 nc.vector.tensor_scalar(out=res[b][:], in0=acc[b][:], scalar1=OUT_SCALE, scalar2=None, op0=ALU.mult)
             else:
                 nc.scalar.activation(out=res[b][:], in_=acc[b][:], func=ACT.Copy, scale=OUT_SCALE)
             nc.sync.dma_start(out=out[b * P : (b + 1) * P, :], in_=res[b][:])
 
+        for b in range(4):
+            nc.tensor.matmul_mx(
+                out=acc[b % RT][:],
+                lhsT=warm_a[:].bitcast(E4M3),
+                lhsT_scale=warm_a_s[:],
+                rhs=warm_b[:].bitcast(E5M2),
+                rhs_scale=warm_b_s[:],
+                start=True,
+                stop=True,
+            )
         for b in range(RT):
             hidden(b)
         weigh(0)
+        cast_rest(0)
         weigh(1)
         quantize_h(0)
-        dst, src = g_views(1, QUARTER, HALF)
-        nc.vector.tensor_copy(out=dst, in_=src)
+        cast_rest(1)
         quantize_g(0)
         quantize_g(1)
-        weigh(2)
         quantize_h(1)
-        quantize_h(2)
+        weigh(2)
         weigh(3)
+        quantize_h(2)
         quantize_h(3)
-        for b in range(RT):
+        for b in range(2):
             stored(b)
+            fresh(b)
+            store(b)
+        for b in range(2, RT):
+            stored(b)
+        for b in range(2, RT):
             fresh(b)
             store(b)

from contextlib import ExitStack

import concourse.mybir as mybir

K, R, T, S, N = 1024, 512, 512, 512, 512
FLOPS = 2 * (K * R * T + T * R * N + S * R * N)

F32 = mybir.dt.float32
BF16 = mybir.dt.bfloat16
I32 = mybir.dt.int32
U8 = mybir.dt.uint8
E4M3 = mybir.dt.float8_e4m3fn_x4
E5M2 = mybir.dt.float8_e5m2_x4
E2M1 = mybir.dt.float4_e2m1fn_x4
ALU = mybir.AluOpType
ACT = mybir.ActivationFunctionType

P = 128
PACK = 4
KP = K // (P * PACK)
RT = R // P
HALF = N // 2
SCALAR_COLS = (192, 128)
OUT_SCALE = 0.04


def load_scales(queue, plane, scales, rows):
    for row in rows:
        queue.dma_start(
            out=plane[row:P:32, :, :].bitcast(I32),
            in_=scales[:, row:16:4, :].rearrange("z q c -> q z c").bitcast(I32),
        )


def tile_mix_wgrad_of_hidden_and_store_kernel(
    tc, xt_words, xt_scales, wa_words, wa_scales, rw, g, hs_words, hs_scales, gs_words, gs_scales, out
):
    nc = tc.nc
    with ExitStack() as ctx:
        sb = ctx.enter_context(tc.tile_pool(name="sb", bufs=1))
        ps = ctx.enter_context(tc.psum_pool(name="ps", bufs=1))
        ctx.enter_context(tc.manual_schedule())

        xs_raw = sb.tile([P, KP, T], U8, align_bytes=64)
        ws = sb.tile([P, KP, R], U8, align_bytes=64)
        stored_s = sb.tile([P, 2, N], U8, align_bytes=64)
        staged = sb.tile([16, 2, N], U8, align_bytes=64)
        nc.gpsimd.dma_start(out=staged[:, 0, :].bitcast(I32), in_=hs_scales[0].bitcast(I32))
        nc.gpsimd.dma_start(out=staged[:, 1, :].bitcast(I32), in_=gs_scales[0].bitcast(I32))
        nc.vector.memset(xs_raw[:].bitcast(I32), 0)
        ones = sb.tile([P, P * PACK], BF16, align_bytes=64)
        warm_a = sb.tile([P, P], I32, align_bytes=64)
        warm_a_s = sb.tile([P, P], U8, align_bytes=64)
        warm_b = sb.tile([P, N], I32, align_bytes=64)
        warm_b_s = sb.tile([P, N], U8, align_bytes=64)
        nc.vector.memset(ones[:], 1.0)
        nc.vector.memset(ws[:].bitcast(I32), 0)
        nc.vector.quantize_mx(out=warm_a[:].bitcast(E4M3), scales=warm_a_s[:], in_=ones[:])
        for c in range(0, N, P):
            nc.vector.quantize_mx(out=warm_b[:, c : c + P].bitcast(E5M2), scales=warm_b_s[:, c : c + P], in_=ones[:])
        nc.vector.memset(stored_s[:].bitcast(I32), 0)

        xt_raw = sb.tile([P, KP, T], I32, align_bytes=64)
        wa = sb.tile([P, KP, 2 * R], U8, align_bytes=64)
        rw_sb = sb.tile([P, 1, PACK], F32, align_bytes=64)
        hs = sb.tile([P, R], I32, align_bytes=64)
        gs = sb.tile([P, 2 * N], U8, align_bytes=64)
        g_raw = [sb.tile([P, PACK, HALF], F32, align_bytes=64, name="g_raw%d" % h) for h in range(2)]
        g_rows = g.rearrange("(p j) n -> p j n", j=PACK)

        load_scales(nc.sync, xs_raw, xt_scales, range(2))
        load_scales(nc.scalar, xs_raw, xt_scales, range(2, 4))
        nc.sync.dma_start(out=xt_raw[:], in_=xt_words.rearrange("z p c b -> p z (c b)").bitcast(I32))
        nc.sync.dma_start(out=wa[:].bitcast(I32), in_=wa_words.rearrange("z p c -> p z c").bitcast(I32))
        load_scales(nc.sync, ws, wa_scales, range(4))
        nc.sync.dma_start(out=rw_sb[:], in_=rw.rearrange("o (p j) -> p o j", j=PACK))
        for h in range(2):
            nc.sync.dma_start(out=g_raw[h][:], in_=g_rows[:, :, h * HALF : (h + 1) * HALF])
        nc.sync.dma_start(out=gs[:].bitcast(I32), in_=gs_words[0].bitcast(I32))
        hs_cols = hs_words[0].rearrange("p c b -> p (c b)").bitcast(I32)
        nc.sync.dma_start(out=hs[:, :P], in_=hs_cols[:, :P])
        for row in range(4):
            nc.sync.dma_start(out=stored_s[row:P:32, :, :].bitcast(I32), in_=staged[row:16:4, :, :].bitcast(I32))
        nc.sync.dma_start(out=hs[:, P:], in_=hs_cols[:, P:])

        xs = sb.tile([P, KP, PACK, P], U8, align_bytes=64)
        nc.vector.tensor_copy(
            out=xs[:].rearrange("p z j (c i) -> p z c j i", i=16),
            in_=xs_raw[:].rearrange("p z (c i j) -> p z c j i", i=16, j=PACK),
        )
        xt = sb.tile([P, KP, PACK, P], I32, align_bytes=64)
        for z in range(KP):
            nc.vector.tensor_copy(
                out=xt[:, z, :, :].rearrange("p j (c i) -> p c j i", i=4),
                in_=xt_raw[:, z, :].rearrange("p (c i j) -> p c j i", i=4, j=PACK),
            )

        g_bf = sb.tile([P, N * PACK], BF16, align_bytes=64)
        gq = sb.tile([P, N], I32, align_bytes=64)
        gq_s = sb.tile([P, N], U8, align_bytes=64)

        def g_views(h, lo, hi):
            first = h * HALF
            return (
                g_bf[:, (first + lo) * PACK : (first + hi) * PACK].rearrange("p (c i j) -> p c j i", i=4, j=PACK),
                g_raw[h][:, :, lo:hi].rearrange("p j (c i) -> p c j i", i=4),
            )

        def quantize_g(h):
            cols = slice(h * HALF, (h + 1) * HALF)
            nc.vector.quantize_mx(
                out=gq[:, cols].bitcast(E5M2),
                scales=gq_s[:, cols],
                in_=g_bf[:, h * HALF * PACK : (h + 1) * HALF * PACK],
            )

        for h in range(2):
            dst, src = g_views(h, 0, SCALAR_COLS[h])
            nc.scalar.activation(out=dst, in_=src, func=ACT.Copy)

        def cast_rest(h):
            dst, src = g_views(h, SCALAR_COLS[h], HALF)
            nc.vector.tensor_copy(out=dst, in_=src)

        pre = [ps.tile([P, PACK, P], F32, name="pre%d" % b) for b in range(RT)]
        acc = [ps.tile([P, N], F32, name="acc%d" % b) for b in range(RT)]
        ht = [sb.tile([P, P, PACK], BF16, align_bytes=64, name="ht%d" % b) for b in range(RT)]
        hq = [sb.tile([P, P], I32, align_bytes=64, name="hq%d" % b) for b in range(RT)]
        hq_s = [sb.tile([P, P], U8, align_bytes=64, name="hq_s%d" % b) for b in range(RT)]
        res = [sb.tile([P, N], F32, align_bytes=64, name="res%d" % b) for b in range(RT)]

        def hidden(b):
            for j in range(PACK):
                for z in range(KP):
                    nc.tensor.matmul_mx(
                        out=pre[b][:, j, :],
                        lhsT=xt[:, z, j, :].bitcast(E4M3),
                        lhsT_scale=xs[:, z, j, :],
                        rhs=wa[:, z, 2 * b * P : 2 * (b + 1) * P].bitcast(E2M1),
                        rhs_scale=ws[:, z, b * P : (b + 1) * P],
                        start=(z == 0),
                        stop=(z == KP - 1),
                    )

        def weigh(b):
            nc.vector.scalar_tensor_tensor(
                out=ht[b][:],
                in0=pre[b][:].rearrange("p j r -> p r j"),
                scalar=0.0,
                in1=rw_sb[:].to_broadcast([P, P, PACK]),
                op0=ALU.max,
                op1=ALU.mult,
            )

        def quantize_h(b):
            nc.vector.quantize_mx(
                out=hq[b][:].bitcast(E4M3), scales=hq_s[b][:], in_=ht[b][:].rearrange("p r j -> p (r j)")
            )

        def stored(b):
            cols = slice(b * P, (b + 1) * P)
            nc.tensor.matmul_mx(
                out=acc[b][:],
                lhsT=hs[:, cols].bitcast(E4M3),
                lhsT_scale=stored_s[:, 0, cols],
                rhs=gs[:].bitcast(E2M1),
                rhs_scale=stored_s[:, 1, :],
                start=True,
                stop=False,
            )

        def fresh(b):
            nc.tensor.matmul_mx(
                out=acc[b][:],
                lhsT=hq[b][:].bitcast(E4M3),
                lhsT_scale=hq_s[b][:],
                rhs=gq[:].bitcast(E5M2),
                rhs_scale=gq_s[:],
                start=False,
                stop=True,
            )

        def store(b):
            if b == RT - 2:
                nc.vector.tensor_scalar(out=res[b][:], in0=acc[b][:], scalar1=OUT_SCALE, scalar2=None, op0=ALU.mult)
            else:
                nc.scalar.activation(out=res[b][:], in_=acc[b][:], func=ACT.Copy, scale=OUT_SCALE)
            nc.sync.dma_start(out=out[b * P : (b + 1) * P, :], in_=res[b][:])

        for b in range(4):
            nc.tensor.matmul_mx(
                out=acc[b % RT][:],
                lhsT=warm_a[:].bitcast(E4M3),
                lhsT_scale=warm_a_s[:],
                rhs=warm_b[:].bitcast(E5M2),
                rhs_scale=warm_b_s[:],
                start=True,
                stop=True,
            )
        for b in range(RT):
            hidden(b)
        weigh(0)
        cast_rest(0)
        weigh(1)
        quantize_h(0)
        cast_rest(1)
        quantize_g(0)
        quantize_g(1)
        quantize_h(1)
        weigh(2)
        weigh(3)
        quantize_h(2)
        quantize_h(3)
        for b in range(2):
            stored(b)
            fresh(b)
            store(b)
        for b in range(2, RT):
            stored(b)
        for b in range(2, RT):
            fresh(b)
            store(b)
